import numpy as np, ml_dtypes
CORES = [5,29,101,125,133,157,229,253]
N = 8
import mx_ref
BF = ml_dtypes.bfloat16
def pick(q, e):
    c = np.concatenate([q[0].reshape(128, -1, 4), np.zeros((128, 1, 4), np.uint8)], axis=1); s = np.concatenate([q[1], np.ones((16, 1), np.uint8)], axis=1)
    return (np.ascontiguousarray(c[:, e].reshape(128, -1)), np.ascontiguousarray(s[:, e]))
def join(*qs):
    return (np.concatenate([q[0] for q in qs], axis=1), np.concatenate([q[1] for q in qs], axis=1))
def put(q, e, v):
    c, s = q[0].reshape(128, -1, 4).copy(), q[1].copy(); c[:, e] = v[0].reshape(128, -1, 4); s[:, e] = v[1]
    return (c.reshape(128, -1), s)
def pk(c, s):
    return (np.ascontiguousarray(c), mx_ref.live(s))
def emit(q):
    return q[0], q[1]
def tile(rs):
    return np.stack(rs, axis=2).reshape(128, -1).astype(BF)
def cut(t, i, w=512):
    return t[:, w * i:w * i + w]
def f(rng, *shape):
    return mx_ref.flush((rng.standard_normal(shape, dtype=np.float32) * np.exp2(rng.integers(-2, 3, shape[:-1] + (1,)))).astype(BF))
def wide(rng, *shape, cols=0):
    v = rng.standard_normal(shape, dtype=np.float32) * np.exp2(rng.integers(-12, 13, shape)).astype(np.float32)
    if cols: v *= np.repeat(np.exp2(rng.integers(-cols, cols + 1, shape[:-2] + (1, shape[-1] // 4))) * (rng.random(shape[:-2] + (1, shape[-1] // 4)) > 0.0625), 4, axis=-1).astype(np.float32)
    return mx_ref.flush(v.astype(BF))
P, CAPP, L, CB = 128, 64, 3, 64
def big(v, k):
    v = v.astype(np.float32) * np.float32(k)
    v[np.abs(v) < np.float32(2.0 ** -10)] = 0
    return v.astype(BF)
def number(z):
    n = np.zeros(z.shape[1], np.int64)
    for b in range(L): n += (z[b] < 0) * (1 << b)
    return n
def buckets(x, pl):
    X = [mx_ref.quantize(np.ascontiguousarray(x[s])) for s in range(N)]
    return X, np.stack([number(mx_ref.matmul(mx_ref.quantize(np.ascontiguousarray(pl[s])), X[s])) for s in range(N)])
def taken(bk):
    at = np.full((N, N, CAPP), -1)
    for d in range(N):
        for s in range(N):
            e = np.flatnonzero(bk[s] == d)[:CAPP]
            at[d, s, :e.size] = e
    return at
def attend(c, wv, e):
    e = np.concatenate([e, np.setdiff1d(np.arange(512), e)[:max(4 - len(e), len(e) % 2)]])
    m = pick(c, e)
    ct = [pick(c, np.arange(t, 512, 4)) for t in range(4)]
    A = tile([np.float32(0.0625) * np.maximum(mx_ref.matmul(k, m) + np.float32(0), np.float32(0)) for k in ct])
    qw = mx_ref.quantize(np.ascontiguousarray(wv))
    V = tile([mx_ref.matmul(k, qw) for k in ct])
    qa = mx_ref.quantize(A)
    O = [mx_ref.matmul(mx_ref.quantize(np.ascontiguousarray(cut(V, i))), qa) for i in range(4)]
    h = np.zeros((128, 512, 4), BF)
    h[:, e] = tile([np.float32(0.0625) * o for o in O]).reshape(128, -1, 4)
    return A, V, h.reshape(128, 2048)
def planes(rng):
    p = np.array(f(rng, 128, 512))
    p[:, 4 * L:] = 0
    return np.stack([p] * N)
def plain(rng):
    return {"x": big(f(rng, N, 128, 4 * P), 0.25), "pl": planes(rng), "p2": planes(rng), "wv": big(f(rng, N, 128, 2048), 0.25), "w": f(rng, N, 128, 512)}
def aimed(rng, d, want, gone=0, then=None, two=None):
    x, p = d["x"].astype(np.float32).reshape(N, 128, P, 4), np.zeros((128, 128, 4), np.float32)
    gone = np.zeros((N, P), np.int64) + gone
    at = rng.permutation(128)[:16 * L + 16].reshape(L + 1, 16)
    side = np.zeros((N, 128, 4), np.float32)
    for b in range(L):
        v = (1 + rng.random((16, 4))) * rng.choice([-1.0, 1.0], (16, 4))
        p[at[b], b] = v
        turn = (1 - 2 * (want >> b & 1)) * (1 - (gone >> b & 1))
        x[:, at[b]] = np.abs(x[:, at[b]]) * (np.sign(v)[None, :, None, :] * turn[:, None, :, None]) * (0.0625 if then is None else 1.0)
        side[:, at[b]] = np.sign(v)[None] * (1 - 2 * (np.arange(N) >> b & 1))[:, None, None]
    parted = np.zeros((128, 4), np.float32)
    if two is not None:
        k = two[2][:, None, :, None]
        u = rng.choice([-1.0, 1.0], (16, 4))
        parted[at[L]] = u
        x = np.where(k != 0, np.float32(0.125) * x, x)
        x[:, at[L]] = np.where(k != 0, 0.5 * (1 + rng.random((N, 16, P, 4))) * u[None, :, None, :] * k, x[:, at[L]])
    x = x * (gone != N - 1)[:, None, :, None]
    d = {**d, "x": big(x.reshape(N, 128, 4 * P), 1), "pl": np.stack([p.reshape(128, 512).astype(BF)] * N)}
    if then is None: return d
    p2, wv = np.zeros((128, 128, 4), np.float32), d["wv"].astype(np.float32).reshape(N, 128, 4, 128, 4)
    on = rng.permutation(128)[:16 * L].reshape(L, 16)
    for b in range(L):
        p2[on[b], b] = 1 + rng.random((16, 4))
        for q in range(N):
            sign = parted if two is not None and q == two[0] and b == two[1] else side[q]
            wv[q][:, :, on[b]] = np.abs(wv[q][:, :, on[b]]) * sign[:, None, None, :] * (1 - 2 * (int(then[q]) >> b & 1))
    return {**d, "wv": big(wv.reshape(N, 128, 2048), 1), "p2": np.stack([p2.reshape(128, 512).astype(BF)] * N)}
def setup_inputs(rng):
    return plain(rng)
def setup_inputs_crowd(rng):
    h, g = (int(v) for v in rng.permutation(N)[:2])
    c, then = rng.permutation(N), np.zeros(N, np.int64)
    then[c] = np.roll(c, 1)
    bit = int(rng.choice([b for b in range(L) if int(then[h]) ^ (1 << b) != h]))
    one = int(rng.choice([q for q in range(N) if q not in (h, g) and int(then[q]) != int(then[h]) ^ (1 << bit)]))
    others = np.delete(np.arange(N), [h, g, one])
    o, n = rng.permutation(N), np.full(N, CAPP)
    n[o[N // 2:]] += rng.integers(1, P - CAPP + 1, N - N // 2)
    n[o[-1]] = P
    r, more = int(o[N // 2]), P // (CAPP + 1) - 1
    if more: n[r] = rng.integers(CAPP + 1, P - more * (CAPP + 1) + 1)
    want = rng.choice(others, (N, P))
    for s in range(N): want[s, rng.permutation(P)[:n[s]]] = h
    e = rng.permutation(np.flatnonzero((want != h) & (np.arange(N) != r)[:, None]))
    want.flat[e[:CB]] = g
    want.flat[e[CB]] = one
    if more:
        e = rng.permutation(np.flatnonzero(want[r] != h))
        want[r, e[:more * (CAPP + 1)]] = np.repeat(rng.choice(others, more, replace=False), CAPP + 1)
    kind = np.zeros((N, P), np.int64)
    for s in range(N):
        e = np.flatnonzero(want[s] == h)
        kind[s, e] = 1 - 2 * ((np.arange(e.size) + int(rng.integers(0, 2))) % 2)
    return aimed(rng, plain(rng), want, then=then, two=(h, bit, kind))
def setup_inputs_few(rng):
    o = rng.permutation(N)
    want = rng.choice(o[2:], (N, P))
    want[int(rng.integers(0, N)), int(rng.integers(0, P))] = o[0]
    return aimed(rng, plain(rng), want)
def setup_inputs_neg(rng):
    d, g = plain(rng), rng.permutation(16)
    want = np.stack([rng.permutation(P) % N for s in range(N)])
    part = 8 * g[:, None] + np.arange(8)
    rows = (4 * part[L:].reshape(-1)[:, None] + np.arange(4)).reshape(-1)
    x, p = np.zeros((N, P, 512)), np.zeros((128, 128, 4))
    for b in range(L):
        v = rng.choice([-1.0, 1.0], (8, 4))
        p[part[b], b] = v * (1 + rng.random((8, 4)))
        e = (4 * part[b][:, None] + np.arange(4)).reshape(-1)
        x[:, :, e] = 2.0 ** -8 * v.reshape(-1) * (1 - 2 * (want >> b & 1))[:, :, None]
    for q in range(N):
        s, i = np.nonzero(want == q)
        v = np.full((P, P), -2.0 ** -7)
        v[np.arange(P), np.arange(P)] = P * 2.0 ** -7
        x[s[:, None], i[:, None], rng.permutation(rows)[:P][None, :]] = v * rng.choice([-1.0, 1.0], P)
    x *= np.exp2(rng.integers(-1, 2, (N, P, 1)))
    x = np.ascontiguousarray(x.reshape(N, P, 128, 4).transpose(0, 2, 1, 3)).reshape(N, 128, 4 * P)
    return {**d, "x": x.astype(np.float32).astype(BF), "pl": np.stack([p.reshape(128, 512).astype(np.float32).astype(BF)] * N)}
def setup_inputs_zero(rng):
    gone = np.zeros((N, P), np.int64)
    for s in range(N):
        e = rng.permutation(P)
        gone[s, e[:P // 4]] = N - 1
        gone[s, e[P // 4:P // 2]] = 1 << rng.integers(0, L, P // 2 - P // 4)
    d = aimed(rng, plain(rng), rng.integers(0, N, (N, P)), gone)
    b, q, on = int(rng.integers(0, L)), int(rng.integers(0, N)), rng.permutation(128)[:16]
    p2, wv = np.array(d["p2"]).reshape(N, 128, 128, 4), np.array(d["wv"]).reshape(N, 128, 4, 128, 4)
    p2[:, np.setdiff1d(np.arange(128), on), b] = 0
    wv[q][:, :, on] = 0
    return {**d, "p2": p2.reshape(N, 128, 512), "wv": wv.reshape(N, 128, 2048)}
def setup_inputs_spread(rng):
    return {**plain(rng), "x": big(wide(rng, N, 128, 4 * P, cols=2), 2.0 ** -10)}
def check_inputs(d):
    b = []
    for k in ("x", "pl", "p2", "wv", "w"):
        v = np.abs(d[k].astype(np.float32))
        if not (np.isfinite(v).all() and ((v == 0) | (v >= 2.0 ** -30) & (v <= 2.0 ** 30)).all()): b.append("a value of " + k)
    for k in ("pl", "p2"):
        p = d[k].astype(np.float32)
        if (p[:, :, 4 * L:] != 0).any(): b.append(k + " has numbers behind its first L columns")
        if (p != p[:1]).any(): b.append(k + " isn't the same on all ranks")
    return b
def reference(x, pl, p2, wv, w):
    X, bk = buckets(x, pl)
    at = taken(bk)
    H, num, to = [], [], []
    for d in range(N):
        c = join(*[pick(X[s], at[d, s]) for s in range(N)])
        A, V, h = attend(c, wv[d], np.flatnonzero(at[d].reshape(-1) >= 0))
        h = mx_ref.quantize(h)
        n = np.concatenate([np.where(at[d, s] >= 0, P * s + at[d, s], -1) for s in range(N)])
        H.append(h)
        num.append(n)
        to.append(np.where(n >= 0, number(mx_ref.matmul(mx_ref.quantize(np.ascontiguousarray(p2[d])), h)), -1))
    H = join(*H)
    num = np.concatenate(num + [np.full(1, -1)])
    oc, osc = np.zeros((N, 128, 4 * N * CB), np.uint8), np.zeros((N, 16, N * CB), np.uint8)
    nb, y = np.zeros((N, 1, N * CB), np.float32), np.zeros((N, 128, N * CB), np.float32)
    for e in range(N):
        k = np.full(N * CB, -1)
        for d in range(N):
            i = np.flatnonzero(to[d] == e)[:CB]
            k[d * CB + np.arange(i.size)] = 512 * d + i
        h = pick(H, k)
        oc[e], osc[e] = emit(h)
        nb[e, 0] = num[k]
        y[e] = mx_ref.matmul(mx_ref.quantize(np.ascontiguousarray(w[e])), h)
    return {"oc": oc, "osc": osc, "id": nb, "y": y}

from concourse.bass import DstId, RemoteDMATransfer
from concourse.mybir import dt, AluOpType as OP, AxisListType, ActivationFunctionType as AF

F8, U8, BF, F32, U16, I32 = "float8_e4m3fn_x4", "uint8", "bfloat16", "float32", "uint16", "int32"
SCRATCH = {"ps": ("psum", [128, 4096], F32)}
for _n, _w in (("xq", 130), ("plq", 128), ("p2q", 128), ("wq", 128), ("wvq", 512), ("sl1r", 256), ("sl1d", 192), ("cl", 512),
               ("cp", 512), ("vq", 512), ("aq", 512), ("hq", 640), ("sl2r", 256), ("sl2d", 192), ("hl", 512),
               ("r1", 64), ("r2", 64)):
    SCRATCH[_n + "c"] = ("sbuf", [128, _w], F8)
    SCRATCH[_n + "s"] = ("sbuf", [128, _w], U8)
for _t, _b in ((BF, "xt 520 plt 512 p2t 512 wt 512 wvt 2048 zt 512 vt 2048 at 2048 ht 2048 vals 256 bs1 128 tr1 128 e1 128 m1 128 "
                    "s1 128 jS 2048 jV 2048 lst1 16 ll1 16 bs2 512 tr2 512 e32 512 e8 128 m2 512 s2 512 t2 512 rr 128 ra 64 rb 32 "
                    "win 784 ta 512 tb 544 wm 34 r1l 2"),
               (F32, "cf 4 wc 8 wcol 8 mE 8 i16 16 u16 8 thr 16 addc 8 kc1 128 l32x 8 i8 8 l4x 8 ic 32 p16 8 iv 256 idu 16 dump 16 "
                     "idc 16 ny1 8 num1 8 x1 32 x1t 32 la 16 lb 16 lf 16 inv 16 idx 512 idrow 520 nx 16 ny 16 num2 16 rc 16 n64 16 "
                     "ov 16 su 16 sv 16 sw 16 x2 32 y2 32 z2 32 idg 512 idt 512 idm 8 idl 8 ysb 512 r2l 1"),
               (U16, "rep1 8 offdb 8 offc 32 offs1 32 sc 16 offs2 32"), (I32, "pI 2 ci 4")):
    _b = _b.split()
    for _i in range(0, len(_b), 2):
        SCRATCH[_b[_i]] = ("sbuf", [128, int(_b[_i + 1])], _t)
SEMAPHORES = ("pv psc pt pg ldx ldpl ldwv ldp2 ldw a1 l1 a2d a2r l2d l2r ls st sts rc1 rs1 rl1 rc2 rs2 rl2").split()


def kmap(topo, cores, s):
    far = [d for d in range(8) if d != s and not topo.may_write(cores[s], cores[d])]
    for w in ((1, 2, 4), (1, 4, 2), (2, 1, 4), (2, 4, 1), (4, 1, 2), (4, 2, 1)):
        for f in range(8):
            k = [sum(w[b] * ((d >> b ^ f >> b) & 1) for b in range(3)) for d in range(8)]
            if k[s] == 7 and all(k[d] < 4 for d in far):
                return w, f, k, [k.index(i) for i in range(8)], far
    raise ValueError("no order of the destinations")


def relays(topo, cores, s):
    far = kmap(topo, cores, s)[4]
    return [c for c in topo.cores_of(cores[s]) if c != cores[s] and all(topo.may_write(c, cores[d]) for d in far)]


def bits(es):
    return sum(1 << e for e in es)


def near_engines(topo, cores, s, d, scales=False):
    es = topo.engines(cores[s], cores[d])
    i = kmap(topo, cores, s)[2][d] - 4
    return ((es[0:4], es[4:6], es[6:8]) if scales else (es[0:2], es[2:4], es[4:8]))[i]


def relay_program(g, core, T, topo):
    C = T.cores
    for s in range(8):
        if core not in topo.cores_of(C[s]):
            continue
        rl = relays(topo, C, s)
        if core not in rl[:4]:
            continue
        d = kmap(topo, C, s)[3][rl.index(core)]
        rid, pid = topo.addr(C[d], core)
        es = topo.engines(core, C[d])

        def go(sem, n, out, src, rsem):
            g.wait_ge(T.sem[sem], n)
            g.remote_dma(out, src, T.sem[rsem], T.sem.ls, pid, rid, bits(es))
        a, b = 64 * s, 64 * s + 64
        go("rc1", 4, T.clc[:, a:b].bitcast(dt.uint8), T.r1c[:, 0:64].bitcast(dt.uint8), "a1")
        go("rs1", 4, T.cls[:, a:b], T.r1s[:, 0:64], "a1")
        go("rl1", 2, T.ll1[:, 2 * s:2 * s + 2], T.r1l[:, 0:2], "l1")
        go("rc2", 4, T.hlc[:, a:b].bitcast(dt.uint8), T.r2c[:, 0:64].bitcast(dt.uint8), "a2r")
        go("rs2", 4, T.hls[:, a:b], T.r2s[:, 0:64], "a2r")
        go("rl2", 2, T.idl[:, s:s + 1], T.r2l[:, 0:1], "l2r")
        g.wait_ge(T.sem.ls, 6 * len(es))


def rank_program(g, core, T, topo):
    me = T.rank_of(core)
    if me is None:
        return relay_program(g, core, T, topo)
    C = T.cores
    w3, flip, kof, dof, far = kmap(topo, C, me)
    near = [d for d in range(8) if d != me and d not in far]
    K0 = sum(w3[b] for b in range(3) if flip >> b & 1)
    rl = relays(topo, C, me)
    Q = {"v": g.vector, "s": g.scalar, "t": g.tensor, "g": g, "y": g.sync}
    SEM = {"v": "pv", "s": "psc", "t": "pt", "g": "pg"}
    cnt, seen = {}, {q: {} for q in Q}

    def W(q, *toks):
        best = {}
        for t in toks:
            best[t[0]] = max(best.get(t[0], 0), t[1])
        for sem in best:
            if seen[q].get(sem, 0) < best[sem]:
                Q[q].wait_ge(T.sem[sem], best[sem])
                seen[q][sem] = best[sem]

    def done(q, inst):
        cnt[q] = cnt.get(q, 0) + 1
        inst.then_inc(T.sem[SEM[q]], 1)
        return (SEM[q], cnt[q])

    def V(inst):
        return done("v", inst)

    def S(inst):
        return done("s", inst)

    def load(q, sem, out, in_):
        cnt[sem] = cnt.get(sem, 0) + 16
        Q[q].dma_start(out, in_).then_inc(T.sem[sem], 16)
        return (sem, cnt[sem])
    v, sc, te = g.vector, g.scalar, g.tensor

    def C1(k, inst):
        return V(inst)

    ldx = load("y", "ldx", T.xt[:, 0:512], T.x[:])
    ldpl = load("s", "ldpl", T.plt[:, 0:128], T.pl[:, 0:128])
    W("y", ldx)
    ldwv = load("y", "ldwv", T.wvt[:], T.wv[:])
    ldp2 = load("y", "ldp2", T.p2t[:, 0:128], T.p2[:, 0:128])
    ldw = load("y", "ldw", T.wt[:], T.w[:])

    fl = {"allow_small_or_imprecise_dtypes": True}
    gi = done("g", g.iota(T.pI[:, 0:1], [[0, 1]], 0, 1))
    done("g", g.iota(T.kc1[:], [[0, 4], [1, 8], [0, 4]], -K0, 0, **fl))
    gi2 = done("g", g.iota(T.i16[:], [[1, 16]], 0, 0, **fl))
    done("g", g.iota(T.i8[:], [[1, 8]], 0, 0, **fl))
    done("g", g.iota(T.ic[:], [[1, 4], [64, 8]], 0, 0, **fl))
    done("g", g.iota(T.iv[:], [[32, 16], [1, 16]], -256, 0, **fl))
    done("g", g.iota(T.idu[:], [[16, 16]], 512, 0, **fl))
    gi3 = done("g", g.iota(T.idc[:], [[128, 8], [0, 2]], 0, 0, **fl))
    zx = V(v.memset(T.xt[:, 512:520], 0.0))
    for b in range(4):
        rep1 = V(v.memset(T.rep1[:, 2 * b:2 * b + 2], b))
    W("v", gi)
    V(v.tensor_scalar(T.ci[:, 0:1], T.pI[:, 0:1], 31, None, OP.bitwise_and))
    V(v.tensor_scalar(T.ci[:, 1:2], T.pI[:, 0:1], 15, None, OP.bitwise_and))
    V(v.tensor_scalar(T.ci[:, 2:3], T.pI[:, 0:1], 4, 1, OP.arith_shift_right, OP.bitwise_and))
    c0 = V(v.tensor_scalar(T.ci[:, 3:4], T.pI[:, 0:1], 3, None, OP.bitwise_and))
    W("v", c0)
    c0 = V(v.tensor_copy(T.cf[:], T.ci[:]))
    W("v", c0)
    lane, l16, mO, u4 = (T.cf[:, i:i + 1] for i in range(4))
    for b in range(3):
        c1 = V(v.tensor_scalar(T.wc[:, b:b + 1], lane, float(b), float(-w3[b] if flip >> b & 1 else w3[b]), OP.is_equal, OP.mult))
    c2 = V(v.tensor_scalar(T.u16[:, 0:1], u4, 16.0, 0.5, OP.mult, OP.add))
    nS = 9
    c3 = V(v.tensor_scalar(T.addc[:, 0:1], l16, nS - 0.5, 64.0, OP.is_lt, OP.mult))
    c4 = V(v.tensor_scalar(T.mE[:, 0:1], mO, -1.0, 1.0, OP.mult, OP.add))
    W("v", c1)
    c1 = V(v.tensor_tensor(T.wc[:, 3:4], T.wc[:, 0:1], T.wc[:, 1:2], OP.add))
    W("v", c1)
    wc = V(v.tensor_tensor(T.wcol[:, 0:1], T.wc[:, 3:4], T.wc[:, 2:3], OP.add))
    W("v", c2, gi2)
    thr = V(v.tensor_scalar(T.thr[:], T.i16[:], T.u16[:, 0:1], None, OP.add))
    wcol, mE = T.wcol[:, 0:1], T.mE[:, 0:1]

    W("v", ldpl)
    for a in range(1, 4):
        k = V(v.tensor_copy(T.plt[:, 128 * a:128 * a + 128], T.plt[:, 0:128]))
    W("v", k)
    qpl = V(v.quantize_mx(T.plqc[:, 0:128], T.plqs[:, 0:128], T.plt[:, 0:512]))
    W("v", ldx, zx)
    qx = V(v.quantize_mx(T.xqc[:, 0:130], T.xqs[:, 0:130], T.xt[:, 0:520]))

    def mm(out, n, l, lo, r, ro):
        return done("t", te.matmul_mx(T.ps[:, out:out + n], T[l + "c"][:, lo:lo + 128], T[l + "s"][:, lo:lo + 128],
                                      T[r + "c"][:, ro:ro + n], T[r + "s"][:, ro:ro + n], True, True))
    W("t", qpl, qx)
    z = mm(0, 128, "plq", 0, "xq", 0)
    W("v", z, wc)
    z1 = V(v.tensor_scalar(T.bs1[:], T.ps[:, 0:128], 0.0, wcol, OP.is_lt, OP.mult))
    W("v", z1)
    k = V(v.transpose(T.tr1[:], T.bs1[:]))
    W("v", k)
    k = V(v.tensor_tensor(T.ny1[:, 0:4], T.tr1[:, 1:128:32], T.tr1[:, 2:128:32], OP.add))
    W("v", k)
    k = V(v.tensor_tensor(T.num1[:, 0:4], T.tr1[:, 0:128:32], T.ny1[:, 0:4], OP.add))
    W("v", k, rep1, gi2)
    k = V(v.tensor_tensor(T.e1[:], T.num1[:, 0:4].indirect(T.rep1[:, 0:8]), T.kc1[:], OP.is_equal))
    W("v", k)
    k = V(v.transpose(T.m1[:], T.e1[:]))
    W("v", k)
    k = V(v.tensor_tensor_scan(T.s1[:], T.m1[:], T.m1[:], 0.0, OP.add, OP.max))
    W("s", k, thr)
    W("v", k, thr)
    for i in range(nS):
        ks = S(sc.activation(T.jS[:, 128 * i:128 * i + 128], T.s1[:], AF.Sign, bias=T.thr[:, i:i + 1], scale=-1.0, accum_out=T.x1[:, i:i + 1]))
    cs = [V(v.tensor_scalar(T.jV[:, 128 * i:128 * i + 128], T.s1[:], T.thr[:, i:i + 1], 2.0, OP.is_lt, OP.mult)) for i in range(nS, 16)]
    for i in range(nS, 16):
        W("v", cs[i - nS])
        k = V(v.tensor_reduce(T.x1[:, i:i + 1], T.jV[:, 128 * i:128 * i + 128], AxisListType.X, OP.add))
    W("v", k, ks)
    k = V(v.tensor_copy(T.x1[:, 16:32], T.x1[:, 0:16]))
    W("v", k)
    k = V(v.transpose(T.x1t[:], T.x1[:]))
    W("v", k, c3)
    of1 = V(v.tensor_scalar(T.offs1[:], T.x1t[:], 0.5, T.addc[:, 0:1], OP.mult, OP.add))
    W("v", of1)
    W("s", of1)

    def pickc(out, a, b, src, n, off, e, f):
        return V(v.tensor_copy(T[out + "c"][:, a:b].bitcast(dt.uint32), T[src + "c"][:, 0:n].bitcast(dt.uint32).indirect(T[off][:, e:f])))

    def picks(out, a, b, src, n, off, e, f):
        return S(sc.activation(T[out + "s"][:, a:b], T[src + "s"][:, 0:n].indirect(T[off][:, e:f]), AF.Copy))
    own = 64 * me
    c1r = pickc("sl1r", 0, 256, "xq", 130, "offs1", 0, 16)
    s1r = picks("sl1r", 0, 256, "xq", 130, "offs1", 0, 16)
    c1d = pickc("sl1d", 0, 192, "xq", 130, "offs1", 16, 28)
    s1d = picks("sl1d", 0, 192, "xq", 130, "offs1", 16, 28)
    c1o = pickc("cl", own, own + 64, "xq", 130, "offs1", 28, 32)
    s1o = picks("cl", own, own + 64, "xq", 130, "offs1", 28, 32)
    W("v", c4)
    V(v.tensor_scalar(T.la[:], T.offs1[:, 0:32:2], mE, None, OP.mult))
    k = V(v.tensor_scalar(T.lb[:], T.offs1[:, 1:32:2], mO, None, OP.mult))
    W("v", k)
    l1 = V(v.tensor_tensor(T.lst1[:], T.la[:], T.lb[:], OP.add))

    lsn = [0]

    def fused(parts):
        tr = []
        for dst, es, s_, d_, sem in parts:
            rid, pid = topo.addr(dst, core)
            tr.append(RemoteDMATransfer(dst_ids=[DstId(rid=rid, pnc=pid)], dma_engine_mask=bits(es), remote_sem=T.sem[sem], srcs=[s_], dsts=[d_]))
            lsn[0] += len(es)
        g.remote_dma_fused(tr, local_sem=T.sem.ls)

    def far_parts(src, dst, sem, lst=False):
        es = [topo.engines(core, c) for c in rl[:4]]
        return [(rl[i], es[i][8 + 2 * i:10 + 2 * i] if lst else es[i][4 * i:4 * i + 4], src(i), dst, sem) for i in range(4)]

    def near_parts(src, dst, sem, scales=False):
        return [(C[dof[4 + i]], near_engines(topo, C, me, dof[4 + i], scales), src(i), dst, sem) for i in range(3)]

    def u8(t, a, b):
        return T[t][:, a:b].bitcast(dt.uint8)
    W("g", c1r)
    fused(far_parts(lambda i: u8("sl1rc", 64 * i, 64 * i + 64), u8("r1c", 0, 64), "rc1"))
    W("g", s1r)
    fused(far_parts(lambda i: T.sl1rs[:, 64 * i:64 * i + 64], T.r1s[:, 0:64], "rs1"))
    W("g", c1d)
    fused(near_parts(lambda i: u8("sl1dc", 64 * i, 64 * i + 64), u8("clc", own, own + 64), "a1"))
    W("g", s1d)
    fused(near_parts(lambda i: T.sl1ds[:, 64 * i:64 * i + 64], T.cls[:, own:own + 64], "a1", True))
    W("g", l1)
    fused(far_parts(lambda i: T.lst1[:, 2 * i:2 * i + 2], T.r1l[:, 0:2], "rl1", True))
    fused(near_parts(lambda i: T.lst1[:, 8 + 2 * i:10 + 2 * i], T.ll1[:, 2 * me:2 * me + 2], "l1"))

    W("v", gi3, c0)
    V(v.tensor_scalar(T.l32x[:, 0:1], l16, 32.0, None, OP.mult))
    V(v.tensor_scalar(T.p16[:, 0:1], mO, 16.0, None, OP.mult))
    k = V(v.tensor_scalar(T.l4x[:, 0:1], l16, 4.0, None, OP.mult))
    W("v", k)
    oc_ = V(v.tensor_scalar(T.offc[:], T.ic[:], T.l4x[:, 0:1], None, OP.add))
    W("v", ldwv)
    qwv = V(v.quantize_mx(T.wvqc[:, 0:512], T.wvqs[:, 0:512], T.wvt[:, 0:2048]))
    V(v.tensor_scalar(T.offdb[:], T.i8[:], T.l32x[:, 0:1], None, OP.add))
    V(v.tensor_scalar(T.vals[:], T.iv[:], T.p16[:, 0:1], None, OP.add))
    V(v.tensor_scalar(T.dump[:], T.idu[:], l16, None, OP.add))
    V(v.memset(T.win[:], 256.0))
    V(v.memset(T.e32[:], 0.0))
    V(v.memset(T.idx[:], 0.0))
    V(v.memset(T.idrow[:, 512:520], -1.0))
    V(v.memset(T.idm[:], 0.0))
    W("v", ldp2)
    for a in range(1, 4):
        V(v.tensor_copy(T.p2t[:, 128 * a:128 * a + 128], T.p2t[:, 0:128]))
    k = V(v.memset(T.zt[:], 0.0))
    W("v", k, ldw)
    V(v.quantize_mx(T.hqc[:, 512:640], T.hqs[:, 512:640], T.zt[:, 0:512]))
    qp2 = V(v.quantize_mx(T.p2qc[:, 0:128], T.p2qs[:, 0:128], T.p2t[:, 0:512]))
    qw = V(v.quantize_mx(T.wqc[:, 0:128], T.wqs[:, 0:128], T.wt[:, 0:512]))

    nd, ndl, nf = 0, 0, 0
    for s in range(8):
        if s in far:
            nf += len(topo.engines(relays(topo, C, s)[kmap(topo, C, s)[2][me]], core))
        elif s != me:
            ndl += len(near_engines(topo, C, s, me))
            nd += len(near_engines(topo, C, s, me)) + len(near_engines(topo, C, s, me, True))
    a1 = ("a1", nd + 2 * nf)
    W("v", a1, c1o, s1o, oc_)
    W("s", a1, c1o, s1o, oc_)
    W("t", a1, c1o, s1o, qwv)
    pc, pp = [], []
    for t in range(4):
        pc.append(pickc("cp", 128 * t, 128 * t + 128, "cl", 512, "offc", 8 * t, 8 * t + 8))
        pp.append(picks("cp", 128 * t, 128 * t + 128, "cl", 512, "offc", 8 * t, 8 * t + 8))
    vc, al, ar = [], [], []
    for t in range(4):
        W("t", pc[t], pp[t], z1)
        m = mm(512 * t, 512, "cp", 128 * t, "wvq", 0)
        W("v", m)
        vc.append(V(v.tensor_copy(T.vt[:, t:2048:4], T.ps[:, 512 * t:512 * t + 512])))
    for h, acc in ((0, al), (1, ar)):
        for t in range(4):
            if h:
                W("t", al[t])
            m = mm(2048 + 512 * t, 256, "cp", 128 * t, "cl", 256 * h)
            W("s", m)
            acc.append(S(sc.activation(T["at"][:, 1024 * h + t:1024 * h + 1024:4], T.ps[:, 2048 + 512 * t:2304 + 512 * t], AF.Relu, scale=0.0625)))
    W("v", *vc)
    qv = V(v.quantize_mx(T.vqc[:, 0:512], T.vqs[:, 0:512], T.vt[:, 0:2048]))
    W("v", *al)
    qa = [V(v.quantize_mx(T.aqc[:, 0:256], T.aqs[:, 0:256], T["at"][:, 0:1024]))]
    W("v", ("l1", ndl + nf), l1)
    if me > 0:
        V(v.tensor_copy(T.lf[:, 0:2 * me], T.ll1[:, 0:2 * me]))
    if me < 7:
        V(v.tensor_copy(T.lf[:, 2 * me + 2:16], T.ll1[:, 2 * me + 2:16]))
    k = V(v.tensor_copy(T.lf[:, 2 * me:2 * me + 2], T.lst1[:, 14:16]))
    W("v", k)
    inv = V(v.tensor_scalar(T.inv[:], T.lf[:], 127.5, 100.0, OP.is_gt, OP.mult))
    kx = V(v.tensor_tensor(T.idx[:, 0:512:32], T.lf[:], T.idc[:], OP.add))
    W("v", *ar)
    qa.append(V(v.quantize_mx(T.aqc[:, 256:512], T.aqs[:, 256:512], T["at"][:, 1024:2048])))
    hc = [[], []]
    for h in range(2):
        for i in range(4):
            W("t", qv, qa[h], vc[i] if h == 0 else ar[i])
            o = 2048 * h + 512 * i
            m = mm(o, 256, "vq", 128 * i, "aq", 256 * h)
            out = T.ht[:, 1024 * h + i:1024 * h + 1024:4]
            if i % 2 == 0:
                W("s", m)
                hc[h].append(S(sc.activation(out, T.ps[:, o:o + 256], AF.Copy, scale=0.0625)))
            else:
                W("v", m)
                hc[h].append(V(v.tensor_scalar(out, T.ps[:, o:o + 256], 0.0625, None, OP.mult)))
        W("v", *hc[h])
        hc[h].append(V(v.quantize_mx(T.hqc[:, 256 * h:256 * h + 256], T.hqs[:, 256 * h:256 * h + 256], T.ht[:, 1024 * h:1024 * h + 1024])))
    for h in range(2):
        W("t", hc[h][4], qp2, hc[0][h])
        m = mm(512 * h, 256, "p2q", 0, "hq", 256 * h)
        W("v", m)
        zb = V(v.tensor_scalar(T.bs2[:, 256 * h:256 * h + 256], T.ps[:, 512 * h:512 * h + 256], 0.0, wcol, OP.is_lt, OP.mult))
        W("v", zb)
        k = V(v.transpose(T.tr2[:, 256 * h:256 * h + 256], T.bs2[:, 256 * h:256 * h + 256]))
    W("v", k, inv)
    V(v.tensor_tensor(T.nx[:], T.tr2[:, 0:512:32], T.inv[:], OP.add))
    k = V(v.tensor_tensor(T.ny[:], T.tr2[:, 1:512:32], T.tr2[:, 2:512:32], OP.add))
    W("v", k)
    k = V(v.tensor_tensor(T.num2[:], T.nx[:], T.ny[:], OP.add))
    W("v", k)
    for i in range(8):
        k = V(v.tensor_scalar(T.e32[:, i:512:32], T.num2[:], float(i - K0), None, OP.is_equal))
    V(v.tensor_scalar(T.n64[:], T.num2[:], 64.0, 64.0 * K0 - 1.0, OP.mult, OP.add))
    W("s", k)
    e8 = S(sc.activation(T.e8[:], T.e32[:].indirect(T.offdb[:, 0:8]), AF.Copy))
    W("v", k)
    k = V(v.transpose(T.m2[:], T.e32[:]))
    W("v", k)
    k = V(v.tensor_tensor_scan(T.s2[:], T.m2[:], T.m2[:], 0.0, OP.add, OP.max))
    W("v", k)
    k = V(v.transpose(T.t2[:], T.s2[:]))
    W("v", k, e8)
    k = V(v.tensor_tensor(T.rr[:], T.t2[:].indirect(T.offdb[:, 0:8]), T.e8[:], OP.mult))
    W("v", k)
    k = V(v.tensor_tensor(T.ra[:], T.rr[:, 0:64], T.rr[:, 64:128], OP.add))
    W("v", k)
    k = V(v.tensor_tensor(T.rb[:], T.ra[:, 0:32], T.ra[:, 32:64], OP.add))
    W("v", k)
    k = V(v.tensor_tensor(T.rc[:], T.rb[:, 0:16], T.rb[:, 16:32], OP.add))
    W("v", k)
    V(v.tensor_scalar(T.ov[:], T.rc[:], 64.5, 5000.0, OP.is_gt, OP.mult))
    k = V(v.tensor_tensor(T.su[:], T.rc[:], T.n64[:], OP.add))
    W("v", k)
    k = V(v.tensor_tensor(T.sv[:], T.su[:], T.ov[:], OP.add))
    W("v", k)
    k = V(v.tensor_tensor(T.sw[:], T.sv[:], T.dump[:], OP.min))
    W("v", k)
    k = V(v.tensor_copy(T.sc[:], T.sw[:]))
    W("v", k)
    k = V(v.tensor_copy(T.win[:, 16:784].indirect(T.sc[:, 0:16]), T.vals[:]))
    W("v", k)
    k = V(v.transpose(T.ta[:], T.win[:, 16:528]))
    k2 = V(v.transpose(T.tb[:], T.win[:, 0:544]))
    W("v", k)
    V(v.tensor_tensor(T.wm[:, 1:33:2], T.ta[:, 0:512:32], T.ta[:, 16:512:32], OP.min))
    W("v", k2)
    k = V(v.tensor_tensor(T.wm[:, 0:33:2], T.tb[:, 0:544:32], T.tb[:, 16:544:32], OP.min))
    W("v", k)
    V(v.tensor_scalar(T.x2[:], T.wm[:, 0:32], mO, None, OP.mult))
    k = V(v.tensor_scalar(T.y2[:], T.wm[:, 1:33], mE, None, OP.mult))
    W("v", k)
    k = V(v.tensor_tensor(T.z2[:], T.x2[:], T.y2[:], OP.add))
    W("v", k)
    of2 = V(v.tensor_scalar(T.offs2[:], T.z2[:], 256.0, None, OP.add))
    W("v", of2)
    W("s", of2, *hc[0], *hc[1])
    c2r = pickc("sl2r", 0, 256, "hq", 514, "offs2", 0, 16)
    s2r = picks("sl2r", 0, 256, "hq", 514, "offs2", 0, 16)
    idr = V(v.transpose(T.idrow[:, 0:512], T.idx[:]))
    c2d = pickc("sl2d", 0, 192, "hq", 514, "offs2", 16, 28)
    s2d = picks("sl2d", 0, 192, "hq", 514, "offs2", 16, 28)
    c2o = pickc("hl", own, own + 64, "hq", 514, "offs2", 28, 32)
    s2o = picks("hl", own, own + 64, "hq", 514, "offs2", 28, 32)
    W("s", idr)
    ig = [S(sc.activation(T.idg[:, 256 * h:256 * h + 256], T.idrow[:].indirect(T.offs2[:, 16 * h:16 * h + 16]), AF.Copy)) for h in range(2)]
    idm = []
    for h in range(2):
        W("v", ig[h])
        k = V(v.transpose(T.idt[:, 256 * h:256 * h + 256], T.idg[:, 256 * h:256 * h + 256]))
        W("v", k)
        V(v.tensor_copy(T.idm[0:32, 4 * h:4 * h + 4], T.idt[0:32, 256 * h:256 * h + 256:64]))
        idm.append(V(v.tensor_copy(T.idm[32:64, 4 * h:4 * h + 4], T.idt[32:64, 256 * h + 32:256 * h + 256:64])))
    W("g", c2r)
    fused(far_parts(lambda i: u8("sl2rc", 64 * i, 64 * i + 64), u8("r2c", 0, 64), "rc2"))
    W("g", s2r)
    fused(far_parts(lambda i: T.sl2rs[:, 64 * i:64 * i + 64], T.r2s[:, 0:64], "rs2"))
    W("g", c2d)
    fused(near_parts(lambda i: u8("sl2dc", 64 * i, 64 * i + 64), u8("hlc", own, own + 64), "a2d"))
    W("g", s2d)
    fused(near_parts(lambda i: T.sl2ds[:, 64 * i:64 * i + 64], T.hls[:, own:own + 64], "a2d", True))
    W("g", idm[0])
    fused(far_parts(lambda i: T.idm[:, i:i + 1], T.r2l[:, 0:1], "rl2", True))
    W("g", idm[1])
    fused(near_parts(lambda i: T.idm[:, 4 + i:5 + i], T.idl[:, me:me + 1], "l2d"))

    def store_oc(d):
        load("y", "st", T.oc[:, 256 * d:256 * d + 256], u8("hlc", 64 * d, 64 * d + 64))

    def store_id(d):
        src = T.idm[0:64, 7:8] if d == me else T.idl[0:64, d:d + 1]
        return load("s", "sts", T["id"][0:1, 64 * d:64 * d + 64], src)
    W("y", c2o, s2o)
    store_oc(me)
    W("y", ("a2d", nd))
    for d in near:
        store_oc(d)
    arr = [("a2d", nd), ("a2r", 2 * nf), c2o, s2o]
    W("t", qw, *arr)
    W("t", hc[0][2], hc[0][3])
    y0 = mm(1024, 256, "wq", 0, "hl", 0)
    y1 = mm(1536, 256, "wq", 0, "hl", 256)
    W("s", y0)
    k0 = S(sc.activation(T.ysb[:, 0:256], T.ps[:, 1024:1280], AF.Copy))
    W("v", y1)
    k1 = V(v.tensor_copy(T.ysb[:, 256:512], T.ps[:, 1536:1792]))
    W("y", *arr)
    for d in far:
        store_oc(d)
    for b in range(4):
        load("y", "st", T.osc[4 * b:4 * b + 4, 0:512], T.hls[32 * b:32 * b + 4, 0:512])
    W("y", k0)
    load("y", "st", T.y[:, 0:256], T.ysb[:, 0:256])
    W("y", k1)
    st = load("y", "st", T.y[:, 256:512], T.ysb[:, 256:512])
    W("s", idm[1], ("l2d", ndl))
    for d in near + [me]:
        store_id(d)
    W("s", ("l2r", nf))
    for d in far:
        sts = store_id(d)
    W("y", st)
    W("s", sts)
    W("g", ("ls", lsn[0]), ("pv", cnt["v"]), ("psc", cnt["s"]), ("pt", cnt["t"]), ("pg", cnt["g"]))
